import numpy as np
import ml_dtypes


def mxq(x, axis, fmt="e4m3"):
    dtype, down = {"e4m3": (ml_dtypes.float8_e4m3fn, 7), "e5m2": (ml_dtypes.float8_e5m2, 14)}[fmt]
    v = np.moveaxis(np.asarray(x, np.float32).astype(ml_dtypes.bfloat16).astype(np.float64), axis, -1)
    blocks = v.reshape(v.shape[:-1] + (-1, 32))
    amax = np.abs(blocks).max(-1, keepdims=True)
    byte = np.maximum(np.where(amax > 0, np.frexp(amax)[1] - 1 + 127, 0) - down, 1)
    scale = np.exp2(byte - 127.0)
    codes = (blocks / scale).astype(np.float32).astype(dtype).astype(np.float64)
    return np.moveaxis((codes * scale).reshape(v.shape), -1, axis)


WIDE = False


def mx_kscale(k):
    if not WIDE:
        return np.ones(k)
    levels = np.array([30, -30])
    if k % 512:
        return np.exp2(np.random.permutation(np.resize(levels, k // 32))).repeat(32)
    a = np.empty((k // 512, 16))
    for p in range(k // 512):
        a[p, :8] = np.random.permutation(np.resize(levels, 8))
        for g in range(8):
            far = levels[np.abs(levels - a[p, g]) >= 10]
            a[p, g + 8] = far[np.random.randint(len(far))]
    return np.exp2(a.ravel()).repeat(32)


def f64(x):
    return np.asarray(x).astype(np.float64)


def striped(idx):
    return np.tile(np.asarray(idx).reshape(-1, 16).T, (8, 1)).astype(np.uint16)


def unstriped(offs):
    return offs[:16].T.reshape(-1).astype(np.int64)


E2M1 = np.array([0.0, 0.5, 1.0, 1.5, 2.0, 3.0, 4.0, 6.0, -0.0, -0.5, -1.0, -1.5, -2.0, -3.0, -4.0, -6.0])


def pack_weight(w, fmt):
    k, n = w.shape
    w = f64(np.asarray(w, np.float32).astype(ml_dtypes.bfloat16)).reshape(k // 32, 32, n)
    amax = np.abs(w).max(1)
    if fmt == "e4m3":
        byte = np.frexp(amax)[1] - 1 + 127 - 7
    else:
        mant, ex = np.frexp(amax / 6.0)
        byte = np.where(mant > 0.5, ex, ex - 1) + 127
    byte = np.clip(np.where(amax > 0, byte, 1), 1, 254)
    scaled = (w * np.exp2(127.0 - byte)[:, None, :]).reshape(k, n).astype(np.float32)
    by_word = np.ascontiguousarray(scaled.reshape(k // 512, 128, 4, n).transpose(0, 1, 3, 2))
    if fmt == "e4m3":
        words = by_word.astype(ml_dtypes.float8_e4m3fn).view(np.uint8)
    else:
        c = by_word.astype(ml_dtypes.float4_e2m1fn).view(np.uint8) & 0xF
        words = (c[..., 0::2] | (c[..., 1::2] << 4)).reshape(k // 512, 128, 2 * n)
    return np.ascontiguousarray(words), np.ascontiguousarray(byte.astype(np.uint8).reshape(k // 512, 16, n))


def unpack_weight(words, scales, fmt):
    g, _, n = scales.shape
    words = np.ascontiguousarray(words).reshape(g, 128, n, -1)
    if fmt == "e4m3":
        vals = words.view(ml_dtypes.float8_e4m3fn).astype(np.float64)
    else:
        nib = np.empty((g, 128, n, 4), np.uint8)
        nib[..., 0::2] = words & 0xF
        nib[..., 1::2] = words >> 4
        vals = E2M1[nib]
    vals = vals * np.repeat(np.exp2(scales.astype(np.float64) - 127.0), 8, axis=1)[..., None]
    return vals.transpose(0, 1, 3, 2).reshape(g * 512, n)


K, T, J, N = 1024, 1024, 256, 256


def setup_inputs():
    n = np.random.standard_normal
    idx = np.random.permutation(T)[:J]
    idx2 = np.random.permutation(T)[:J]
    fk = mx_kscale(K)
    xtp = pack_weight(n((K, T)) * np.random.uniform(0.4, 1.6, (1, T)) / fk[:, None], "e2m1")
    wap = pack_weight(n((K, N)) * 1 / np.sqrt(K) * fk[:, None], "e2m1")
    return {
        "xt_words": xtp[0],
        "xt_scales": xtp[1],
        "wa_words": wap[0],
        "wa_scales": wap[1],
        "wb": (n((K, N)) * 1 / np.sqrt(K) * fk[:, None]).astype(np.float32),
        "bi": (np.random.uniform(-0.6, 0.6, (1, N))).astype(np.float32),
        "offs": striped(idx),
        "offs2": striped(idx2),
    }


def reference(xt_words, xt_scales, wa_words, wa_scales, wb, bi, offs, offs2):
    idx = unstriped(offs)
    idx2 = unstriped(offs2)
    xtu = unpack_weight(xt_words, xt_scales, "e2m1")
    wau = unpack_weight(wa_words, wa_scales, "e2m1")
    xtidxg = xtu[:, idx]
    a = xtidxg.T @ wau
    xtidx2g = xtu[:, idx2]
    wbq = mxq(f64(wb), 0, "e5m2")
    b0 = xtidx2g.T @ wbq
    b2 = b0 + f64(bi)
    e = np.exp(0.6 * (a - b2))
    y = 256.0 * e / np.sum(e, axis=1, keepdims=True)
    return y

@@ -1,0 +1,152 @@
+from contextlib import ExitStack
+
+import concourse.mybir as mybir
+from concourse.masks import make_identity
+
+K, T, J, N = 1024, 1024, 256, 256
+FLOPS = 2 * 2 * K * J * N
+
+F32 = mybir.dt.float32
+BF16 = mybir.dt.bfloat16
+I32 = mybir.dt.int32
+U32 = mybir.dt.uint32
+U16 = mybir.dt.uint16
+U8 = mybir.dt.uint8
+FP4X4 = mybir.dt.float4_e2m1fn_x4
+E5M2X4 = mybir.dt.float8_e5m2_x4
+ALU = mybir.AluOpType
+ACT = mybir.ActivationFunctionType
+
+P = 128
+PACK = 4
+PASSES = K // (P * PACK)
+QUADS = 4
+ROWS = 4
+RUN = 4
+GAP = 0.6
+TOTAL = 256.0
+
+
+def tile_list_rows_twotokens_sharesofgap_kernel(tc, xt_words, xt_scales, wa_words, wa_scales, wb, bi, offs, offs2, out):
+    nc = tc.nc
+    with ExitStack() as ctx:
+        sb = ctx.enter_context(tc.tile_pool(name="sb", bufs=1))
+        ps = ctx.enter_context(tc.psum_pool(name="ps", bufs=1))
+
+        lists = [sb.tile([P, J // 16], U16, name="list%d" % i) for i in range(2)]
+        xw = [sb.tile([P, T], U16, name="xw%d" % z, align_bytes=64) for z in range(PASSES)]
+        xs = sb.tile([P, PASSES, T], U8, align_bytes=64)
+        waw = sb.tile([P, PASSES, 2 * N], U8, align_bytes=64)
+        was = sb.tile([P, PASSES, N], U8, align_bytes=64)
+        wraw = [sb.tile([P, PACK, N], F32, name="wraw%d" % z, align_bytes=64) for z in range(PASSES)]
+        bcol = sb.tile([P, 2], F32)
+        ident = sb.tile([P, P], F32, align_bytes=64)
+
+        nc.vector.memset(xs[:].rearrange("p z c -> p (z c)").bitcast(I32), 0)
+        nc.gpsimd.memset(was[:].rearrange("p z c -> p (z c)").bitcast(I32), 0)
+        make_identity(nc, ident[:])
+
+        def load_xw(z):
+            nc.sync.dma_start(out=xw[z][:].bitcast(I32), in_=xt_words[z].bitcast(I32))
+
+        def load_wb(z):
+            rows = wb[z * P * PACK : (z + 1) * P * PACK, :]
+            nc.sync.dma_start(out=wraw[z][:], in_=rows.rearrange("(p t) n -> p t n", t=PACK))
+
+        def load_scales(queue, plane, src):
+            for q in range(QUADS):
+                queue.dma_start(
+                    out=plane[32 * q : 32 * q + ROWS, :, :].bitcast(I32),
+                    in_=src[:, ROWS * q : ROWS * (q + 1), :].rearrange("z r c -> r z c").bitcast(I32),
+                )
+
+        nc.sync.dma_start(lists[0][:], offs)
+        load_xw(0)
+        nc.sync.dma_start(lists[1][:], offs2)
+        load_scales(nc.scalar, xs, xt_scales)
+        load_wb(0)
+        load_xw(1)
+        load_wb(1)
+        nc.sync.dma_start(out=waw[:].bitcast(I32), in_=wa_words.rearrange("z p c -> p z c").bitcast(I32))
+        nc.sync.dma_start(out=bcol[:], in_=bi.rearrange("o (p c) -> (o p) c", c=2))
+        load_scales(nc.sync, was, wa_scales)
+
+        gw = [[sb.tile([P, J], U16, name="gw%d%d" % (i, z), align_bytes=64) for z in range(PASSES)] for i in range(2)]
+        gs = [[sb.tile([P, J], U8, name="gs%d%d" % (i, z), align_bytes=64) for z in range(PASSES)] for i in range(2)]
+        wbf = [sb.tile([P, N, PACK], BF16, name="wbf%d" % z, align_bytes=64) for z in range(PASSES)]
+        wq = [sb.tile([P, N], U32, name="wq%d" % z, align_bytes=64) for z in range(PASSES)]
+        wqs = [sb.tile([P, N], U8, name="wqs%d" % z, align_bytes=64) for z in range(PASSES)]
+
+        def gather_words(z):
+            for i in range(2):
+                nc.vector.tensor_copy(gw[i][z][:], xw[z][:].indirect(lists[i][:]))
+
+        def gather_scales(z):
+            for i in range(2):
+                nc.vector.tensor_copy(gs[i][z][:], xs[:, z, :].indirect(lists[i][:]))
+
+        def round_wb(z):
+            nc.scalar.activation(
+                out=wbf[z][:].rearrange("p (c i) t -> p c t i", i=RUN),
+                in_=wraw[z][:].rearrange("p t (c i) -> p c t i", i=RUN),
+                func=ACT.Copy,
+                scale=-1.0,
+            )
+
+        def quantize_wb(z):
+            nc.vector.quantize_mx(
+                out=wq[z][:].bitcast(E5M2X4), scales=wqs[z][:], in_=wbf[z][:].rearrange("p n t -> p (n t)")
+            )
+
+        round_wb(0)
+        round_wb(1)
+        gather_words(0)
+        gather_scales(0)
+        gather_scales(1)
+        gather_words(1)
+        quantize_wb(0)
+        quantize_wb(1)
+
+        bias_ps = ps.tile([P, 2, P], F32)
+        for c in range(2):
+            nc.tensor.transpose(bias_ps[:, c, :], bcol[:, c : c + 1].to_broadcast([P, P]), ident[:])
+        bias = sb.tile([P, P, 2], F32)
+        nc.scalar.activation(out=bias[:], in_=bias_ps[:].rearrange("p c k -> p k c"), func=ACT.Copy, scale=GAP)
+
+        gap = [ps.tile([P, N], F32, name="gap%d" % h) for h in range(J // P)]
+        steps = [(0, 0), (0, 1), (1, 0), (1, 1)]
+        for s, (i, z) in enumerate(steps):
+            for h in range(J // P):
+                cols = slice(h * P, (h + 1) * P)
+                if i == 0:
+                    rhs, rhs_scale = waw[:, z, :].bitcast(FP4X4), was[:, z, :]
+                else:
+                    rhs, rhs_scale = wq[z][:].bitcast(E5M2X4), wqs[z][:]
+                nc.tensor.matmul_mx(
+                    out=gap[h][:],
+                    lhsT=gw[i][z][:, cols].bitcast(FP4X4),
+                    lhsT_scale=gs[i][z][:, cols],
+                    rhs=rhs,
+                    rhs_scale=rhs_scale,
+                    start=(s == 0),
+                    stop=(s == len(steps) - 1),
+                )
+
+        neg = [sb.tile([P, N], F32, name="neg%d" % h) for h in range(J // P)]
+        low = [sb.tile([P, 1], F32, name="low%d" % h) for h in range(J // P)]
+        for h in range(J // P):
+            nc.vector.scalar_tensor_tensor(
+                out=neg[h][:], in0=gap[h][:], scalar=-GAP, in1=bias[:].rearrange("p k c -> p (k c)"),
+                op0=ALU.mult, op1=ALU.add,
+            )
+        for h in range(J // P):
+            nc.vector.tensor_reduce(out=low[h][:], in_=neg[h][:], axis=mybir.AxisListType.X, op=ALU.min)
+        for h in range(J // P):
+            e = sb.tile([P, N], F32, name="e%d" % h)
+            total = sb.tile([P, 1], F32, name="total%d" % h)
+            inv = sb.tile([P, 1], F32, name="inv%d" % h)
+            y = sb.tile([P, N], F32, name="y%d" % h)
+            nc.scalar.activation(out=e[:], in_=neg[h][:], func=ACT.Exp, bias=low[h][:], scale=-1.0, accum_out=total[:])
+            nc.vector.reciprocal(out=inv[:], in_=total[:])
+            nc.vector.tensor_scalar(out=y[:], in0=e[:], scalar1=inv[:], scalar2=TOTAL, op0=ALU.mult, op1=ALU.mult)
+            nc.sync.dma_start(out=out[h * P : (h + 1) * P, :], in_=y[:])

@@ -1,7 +1,6 @@
 from contextlib import ExitStack
 
 import concourse.mybir as mybir
-from concourse.masks import make_identity
 
 K, T, J, N = 1024, 1024, 256, 256
 FLOPS = 2 * 2 * K * J * N
@@ -34,47 +33,52 @@ def tile_list_rows_twotokens_sharesofgap_kernel(tc, xt_words, xt_scales, wa_word
         ps = ctx.enter_context(tc.psum_pool(name="ps", bufs=1))
 
         lists = [sb.tile([P, J // 16], U16, name="list%d" % i) for i in range(2)]
-        xw = [sb.tile([P, T], U16, name="xw%d" % z, align_bytes=64) for z in range(PASSES)]
         xs = sb.tile([P, PASSES, T], U8, align_bytes=64)
         waw = sb.tile([P, PASSES, 2 * N], U8, align_bytes=64)
-        was = sb.tile([P, PASSES, N], U8, align_bytes=64)
-        wraw = [sb.tile([P, PACK, N], F32, name="wraw%d" % z, align_bytes=64) for z in range(PASSES)]
-        bcol = sb.tile([P, 2], F32)
-        ident = sb.tile([P, P], F32, align_bytes=64)
+        bcol = sb.tile([P, 2], F32, tag="small", align_bytes=64)
+        ones = sb.tile([P, P], F32, tag="early", align_bytes=64)
+        ident = sb.tile([P, P], F32, tag="late", align_bytes=64)
 
         nc.vector.memset(xs[:].rearrange("p z c -> p (z c)").bitcast(I32), 0)
-        nc.gpsimd.memset(was[:].rearrange("p z c -> p (z c)").bitcast(I32), 0)
-        make_identity(nc, ident[:])
+        nc.gpsimd.memset(ones[:], 1.0)
+        nc.gpsimd.affine_select(
+            out=ident[:], in_=ones[:], compare_op=ALU.is_equal, fill=0.0, base=0, pattern=[[-1, P]], channel_multiplier=1
+        )
 
-        def load_xw(z):
-            nc.sync.dma_start(out=xw[z][:].bitcast(I32), in_=xt_words[z].bitcast(I32))
+        def load_xw(z, tag):
+            tile = sb.tile([P, T], U16, name="xw%d" % z, tag=tag, align_bytes=64)
+            nc.sync.dma_start(out=tile[:].bitcast(I32), in_=xt_words[z].bitcast(I32))
+            return tile
 
-        def load_wb(z):
-            rows = wb[z * P * PACK : (z + 1) * P * PACK, :]
-            nc.sync.dma_start(out=wraw[z][:], in_=rows.rearrange("(p t) n -> p t n", t=PACK))
-
-        def load_scales(queue, plane, src):
+        def load_scales(plane, src):
             for q in range(QUADS):
-                queue.dma_start(
+                nc.sync.dma_start(
                     out=plane[32 * q : 32 * q + ROWS, :, :].bitcast(I32),
                     in_=src[:, ROWS * q : ROWS * (q + 1), :].rearrange("z r c -> r z c").bitcast(I32),
                 )
 
         nc.sync.dma_start(lists[0][:], offs)
-        load_xw(0)
         nc.sync.dma_start(lists[1][:], offs2)
-        load_scales(nc.scalar, xs, xt_scales)
-        load_wb(0)
-        load_xw(1)
-        load_wb(1)
-        nc.sync.dma_start(out=waw[:].bitcast(I32), in_=wa_words.rearrange("z p c -> p z c").bitcast(I32))
+        xw = [load_xw(0, "xw0")]
         nc.sync.dma_start(out=bcol[:], in_=bi.rearrange("o (p c) -> (o p) c", c=2))
-        load_scales(nc.sync, was, wa_scales)
+        nc.sync.dma_start(out=waw[:].bitcast(I32), in_=wa_words.rearrange("z p c -> p z c").bitcast(I32))
+        load_scales(xs, xt_scales)
+        wraw = sb.tile([P, PASSES, PACK, N], F32, tag="early", align_bytes=64)
+        for z in range(PASSES):
+            rows = wb[z * P * PACK : (z + 1) * P * PACK, :]
+            nc.sync.dma_start(out=wraw[:, z, :, :], in_=rows.rearrange("(p t) n -> p t n", t=PACK))
+
+        bias_ps = ps.tile([P, 2, P], F32)
+        for c in range(2):
+            nc.tensor.transpose(bias_ps[:, c, :], bcol[:, c : c + 1].to_broadcast([P, P]), ident[:])
+        xw.append(load_xw(1, "late"))
+        was = sb.tile([P, PASSES, N], U8, tag="small", align_bytes=64)
+        nc.gpsimd.memset(was[:].rearrange("p z c -> p (z c)").bitcast(I32), 0)
+        load_scales(was, wa_scales)
 
         gw = [[sb.tile([P, J], U16, name="gw%d%d" % (i, z), align_bytes=64) for z in range(PASSES)] for i in range(2)]
         gs = [[sb.tile([P, J], U8, name="gs%d%d" % (i, z), align_bytes=64) for z in range(PASSES)] for i in range(2)]
         wbf = [sb.tile([P, N, PACK], BF16, name="wbf%d" % z, align_bytes=64) for z in range(PASSES)]
-        wq = [sb.tile([P, N], U32, name="wq%d" % z, align_bytes=64) for z in range(PASSES)]
         wqs = [sb.tile([P, N], U8, name="wqs%d" % z, align_bytes=64) for z in range(PASSES)]
 
         def gather_words(z):
@@ -88,33 +92,31 @@ def tile_list_rows_twotokens_sharesofgap_kernel(tc, xt_words, xt_scales, wa_word
         def round_wb(z):
             nc.scalar.activation(
                 out=wbf[z][:].rearrange("p (c i) t -> p c t i", i=RUN),
-                in_=wraw[z][:].rearrange("p t (c i) -> p c t i", i=RUN),
+                in_=wraw[:, z, :, :].rearrange("p t (c i) -> p c t i", i=RUN),
                 func=ACT.Copy,
                 scale=-1.0,
             )
 
-        def quantize_wb(z):
+        def quantize_wb(z, tag):
+            codes = sb.tile([P, N], U32, name="wq%d" % z, tag=tag, align_bytes=64)
             nc.vector.quantize_mx(
-                out=wq[z][:].bitcast(E5M2X4), scales=wqs[z][:], in_=wbf[z][:].rearrange("p n t -> p (n t)")
+                out=codes[:].bitcast(E5M2X4), scales=wqs[z][:], in_=wbf[z][:].rearrange("p n t -> p (n t)")
             )
+            return codes
 
         round_wb(0)
         round_wb(1)
+        bias = sb.tile([P, P, 2], F32, tag="early", align_bytes=64)
+        nc.scalar.activation(out=bias[:], in_=bias_ps[:].rearrange("p c k -> p k c"), func=ACT.Copy, scale=GAP)
         gather_words(0)
         gather_scales(0)
         gather_scales(1)
+        wq = [quantize_wb(0, "wq0")]
         gather_words(1)
-        quantize_wb(0)
-        quantize_wb(1)
-
-        bias_ps = ps.tile([P, 2, P], F32)
-        for c in range(2):
-            nc.tensor.transpose(bias_ps[:, c, :], bcol[:, c : c + 1].to_broadcast([P, P]), ident[:])
-        bias = sb.tile([P, P, 2], F32)
-        nc.scalar.activation(out=bias[:], in_=bias_ps[:].rearrange("p c k -> p k c"), func=ACT.Copy, scale=GAP)
+        wq.append(quantize_wb(1, "late"))
 
         gap = [ps.tile([P, N], F32, name="gap%d" % h) for h in range(J // P)]
-        steps = [(0, 0), (0, 1), (1, 0), (1, 1)]
+        steps = [(1, 0), (0, 0), (0, 1), (1, 1)]
         for s, (i, z) in enumerate(steps):
             for h in range(J // P):
                 cols = slice(h * P, (h + 1) * P)

@@ -1,6 +1,7 @@
 from contextlib import ExitStack
 
 import concourse.mybir as mybir
+from concourse.masks import make_identity
 
 K, T, J, N = 1024, 1024, 256, 256
 FLOPS = 2 * 2 * K * J * N
@@ -33,87 +34,91 @@ def tile_list_rows_twotokens_sharesofgap_kernel(tc, xt_words, xt_scales, wa_word
         ps = ctx.enter_context(tc.psum_pool(name="ps", bufs=1))
 
         lists = [sb.tile([P, J // 16], U16, name="list%d" % i) for i in range(2)]
-        xs = sb.tile([P, PASSES, T], U8, align_bytes=64)
+        xw = [sb.tile([P, T], U16, name="xw%d" % z, align_bytes=64) for z in range(PASSES)]
+        xs = sb.tile([P, T], U8, tag="xs", align_bytes=64)
+        moved = sb.tile([P, 2 * J], U8, align_bytes=64)
         waw = sb.tile([P, PASSES, 2 * N], U8, align_bytes=64)
-        bcol = sb.tile([P, 2], F32, tag="small", align_bytes=64)
-        ones = sb.tile([P, P], F32, tag="early", align_bytes=64)
-        ident = sb.tile([P, P], F32, tag="late", align_bytes=64)
+        was = sb.tile([P, PASSES, N], U8, align_bytes=64)
+        wraw = [sb.tile([P, PACK, N], F32, name="wraw%d" % z, align_bytes=64) for z in range(PASSES)]
+        bcol = sb.tile([P, 2], F32)
+        ident = sb.tile([P, P], F32, align_bytes=64)
 
-        nc.vector.memset(xs[:].rearrange("p z c -> p (z c)").bitcast(I32), 0)
-        nc.gpsimd.memset(ones[:], 1.0)
-        nc.gpsimd.affine_select(
-            out=ident[:], in_=ones[:], compare_op=ALU.is_equal, fill=0.0, base=0, pattern=[[-1, P]], channel_multiplier=1
-        )
-
-        def load_xw(z, tag):
-            tile = sb.tile([P, T], U16, name="xw%d" % z, tag=tag, align_bytes=64)
-            nc.sync.dma_start(out=tile[:].bitcast(I32), in_=xt_words[z].bitcast(I32))
-            return tile
-
-        def load_scales(plane, src):
-            for q in range(QUADS):
-                nc.sync.dma_start(
-                    out=plane[32 * q : 32 * q + ROWS, :, :].bitcast(I32),
-                    in_=src[:, ROWS * q : ROWS * (q + 1), :].rearrange("z r c -> r z c").bitcast(I32),
-                )
-
-        nc.sync.dma_start(lists[0][:], offs)
-        nc.sync.dma_start(lists[1][:], offs2)
-        xw = [load_xw(0, "xw0")]
-        nc.sync.dma_start(out=bcol[:], in_=bi.rearrange("o (p c) -> (o p) c", c=2))
-        nc.sync.dma_start(out=waw[:].bitcast(I32), in_=wa_words.rearrange("z p c -> p z c").bitcast(I32))
-        load_scales(xs, xt_scales)
-        wraw = sb.tile([P, PASSES, PACK, N], F32, tag="early", align_bytes=64)
-        for z in range(PASSES):
-            rows = wb[z * P * PACK : (z + 1) * P * PACK, :]
-            nc.sync.dma_start(out=wraw[:, z, :, :], in_=rows.rearrange("(p t) n -> p t n", t=PACK))
-
-        bias_ps = ps.tile([P, 2, P], F32)
-        for c in range(2):
-            nc.tensor.transpose(bias_ps[:, c, :], bcol[:, c : c + 1].to_broadcast([P, P]), ident[:])
-        xw.append(load_xw(1, "late"))
-        was = sb.tile([P, PASSES, N], U8, tag="small", align_bytes=64)
+        nc.vector.memset(xs[:].bitcast(I32), 0)
+        nc.vector.memset(moved[:].bitcast(I32), 0)
         nc.gpsimd.memset(was[:].rearrange("p z c -> p (z c)").bitcast(I32), 0)
-        load_scales(was, wa_scales)
+        make_identity(nc, ident[:])
 
-        gw = [[sb.tile([P, J], U16, name="gw%d%d" % (i, z), align_bytes=64) for z in range(PASSES)] for i in range(2)]
-        gs = [[sb.tile([P, J], U8, name="gs%d%d" % (i, z), align_bytes=64) for z in range(PASSES)] for i in range(2)]
-        wbf = [sb.tile([P, N, PACK], BF16, name="wbf%d" % z, align_bytes=64) for z in range(PASSES)]
+        def load_xw(z):
+            nc.sync.dma_start(out=xw[z][:].bitcast(I32), in_=xt_words[z].bitcast(I32))
+
+        def load_wb(z):
+            rows = wb[z * P * PACK : (z + 1) * P * PACK, :]
+            nc.sync.dma_start(out=wraw[z][:], in_=rows.rearrange("(p t) n -> p t n", t=PACK))
+
+        nc.sync.dma_start(lists[1][:], offs2)
+        load_xw(0)
+        nc.sync.dma_start(lists[0][:], offs)
+        for q in range(QUADS):
+            nc.sync.dma_start(
+                out=xs[32 * q : 32 * q + PASSES * ROWS, :].bitcast(I32),
+                in_=xt_scales[:, ROWS * q : ROWS * (q + 1), :].bitcast(I32),
+            )
+        load_wb(0)
+        nc.sync.dma_start(out=bcol[:], in_=bi.rearrange("o (p c) -> (o p) c", c=2))
+        load_xw(1)
+        load_wb(1)
+        nc.sync.dma_start(out=waw[:].bitcast(I32), in_=wa_words.rearrange("z p c -> p z c").bitcast(I32))
+        for q in range(QUADS):
+            nc.gpsimd.dma_start(
+                out=was[32 * q : 32 * q + ROWS, :, :].bitcast(I32),
+                in_=wa_scales[:, ROWS * q : ROWS * (q + 1), :].rearrange("z r c -> r z c").bitcast(I32),
+            )
+
+        gw = [[None, None], [None, None]]
+        picked = sb.tile([P, 2 * J], U8, align_bytes=64)
+        planes = [picked, moved]
+        wbf = [sb.tile([P, N, PACK], BF16, name="wbf%d" % z, tag="wbf%d" % z, align_bytes=64) for z in range(PASSES)]
+        wq = [sb.tile([P, N], U32, name="wq%d" % z, align_bytes=64) for z in range(PASSES)]
         wqs = [sb.tile([P, N], U8, name="wqs%d" % z, align_bytes=64) for z in range(PASSES)]
 
-        def gather_words(z):
-            for i in range(2):
-                nc.vector.tensor_copy(gw[i][z][:], xw[z][:].indirect(lists[i][:]))
-
-        def gather_scales(z):
-            for i in range(2):
-                nc.vector.tensor_copy(gs[i][z][:], xs[:, z, :].indirect(lists[i][:]))
+        def gather_words(i, z, tag):
+            gw[i][z] = sb.tile([P, J], U16, name="gw%d%d" % (i, z), tag=tag, align_bytes=64)
+            nc.vector.tensor_copy(gw[i][z][:], xw[z][:].indirect(lists[i][:]))
 
         def round_wb(z):
             nc.scalar.activation(
                 out=wbf[z][:].rearrange("p (c i) t -> p c t i", i=RUN),
-                in_=wraw[:, z, :, :].rearrange("p t (c i) -> p c t i", i=RUN),
+                in_=wraw[z][:].rearrange("p t (c i) -> p c t i", i=RUN),
                 func=ACT.Copy,
                 scale=-1.0,
             )
 
-        def quantize_wb(z, tag):
-            codes = sb.tile([P, N], U32, name="wq%d" % z, tag=tag, align_bytes=64)
+        def quantize_wb(z):
             nc.vector.quantize_mx(
-                out=codes[:].bitcast(E5M2X4), scales=wqs[z][:], in_=wbf[z][:].rearrange("p n t -> p (n t)")
+                out=wq[z][:].bitcast(E5M2X4), scales=wqs[z][:], in_=wbf[z][:].rearrange("p n t -> p (n t)")
             )
-            return codes
 
         round_wb(0)
         round_wb(1)
-        bias = sb.tile([P, P, 2], F32, tag="early", align_bytes=64)
+        gather_words(1, 0, "gw10")
+        for i in range(2):
+            nc.vector.tensor_copy(picked[:, i * J : (i + 1) * J], xs[:].indirect(lists[i][:]))
+        for q in range(QUADS):
+            nc.sync.dma_start(
+                out=moved[32 * q : 32 * q + ROWS, :].bitcast(I32),
+                in_=picked[32 * q + ROWS : 32 * q + 2 * ROWS, :].bitcast(I32),
+            )
+        gather_words(0, 0, "xs")
+        quantize_wb(0)
+        gather_words(0, 1, "wbf0")
+        gather_words(1, 1, "gw11")
+        quantize_wb(1)
+
+        bias_ps = ps.tile([P, 2, P], F32)
+        for c in range(2):
+            nc.tensor.transpose(bias_ps[:, c, :], bcol[:, c : c + 1].to_broadcast([P, P]), ident[:])
+        bias = sb.tile([P, P, 2], F32)
         nc.scalar.activation(out=bias[:], in_=bias_ps[:].rearrange("p c k -> p k c"), func=ACT.Copy, scale=GAP)
-        gather_words(0)
-        gather_scales(0)
-        gather_scales(1)
-        wq = [quantize_wb(0, "wq0")]
-        gather_words(1)
-        wq.append(quantize_wb(1, "late"))
 
         gap = [ps.tile([P, N], F32, name="gap%d" % h) for h in range(J // P)]
         steps = [(1, 0), (0, 0), (0, 1), (1, 1)]
@@ -127,7 +132,7 @@ def tile_list_rows_twotokens_sharesofgap_kernel(tc, xt_words, xt_scales, wa_word
                 nc.tensor.matmul_mx(
                     out=gap[h][:],
                     lhsT=gw[i][z][:, cols].bitcast(FP4X4),
-                    lhsT_scale=gs[i][z][:, cols],
+                    lhsT_scale=planes[z][:, i * J + h * P : i * J + (h + 1) * P],
                     rhs=rhs,
                     rhs_scale=rhs_scale,
                     start=(s == 0),

@@ -20,140 +20,165 @@ ACT = mybir.ActivationFunctionType
 P = 128
 PACK = 4
 PASSES = K // (P * PACK)
-QUADS = 4
+QUAD = 32
+QUADS = P // QUAD
 ROWS = 4
 RUN = 4
-GAP = 0.6
-TOTAL = 256.0
+PER = N // P
+TILES = J // P
+A, B = 0, 1
+GAP_SCALE = 0.6
+SHARE_SUM = 256.0
 
 
-def tile_list_rows_twotokens_sharesofgap_kernel(tc, xt_words, xt_scales, wa_words, wa_scales, wb, bi, offs, offs2, out):
+def tile_list_rows_twotokens_sharesofgap_kernel(
+    tc, xt_words, xt_scales, wa_words, wa_scales, wb, bi, offs, offs2, out
+):
     nc = tc.nc
     with ExitStack() as ctx:
         sb = ctx.enter_context(tc.tile_pool(name="sb", bufs=1))
         ps = ctx.enter_context(tc.psum_pool(name="ps", bufs=1))
 
-        lists = [sb.tile([P, J // 16], U16, name="list%d" % i) for i in range(2)]
-        xw = [sb.tile([P, T], U16, name="xw%d" % z, align_bytes=64) for z in range(PASSES)]
-        xs = sb.tile([P, T], U8, tag="xs", align_bytes=64)
+        lists = [sb.tile([P, J // 16], U16, name="list%d" % i) for i in (A, B)]
+        x_words = [sb.tile([P, T], U16, name="x_words%d" % z, align_bytes=64) for z in range(PASSES)]
+        x_scales = sb.tile([P, T], U8, tag="x_scales", align_bytes=64)
         moved = sb.tile([P, 2 * J], U8, align_bytes=64)
-        waw = sb.tile([P, PASSES, 2 * N], U8, align_bytes=64)
-        was = sb.tile([P, PASSES, N], U8, align_bytes=64)
-        wraw = [sb.tile([P, PACK, N], F32, name="wraw%d" % z, align_bytes=64) for z in range(PASSES)]
-        bcol = sb.tile([P, 2], F32)
+        a_words = sb.tile([P, PASSES, 2 * N], U8, align_bytes=64)
+        a_planes = sb.tile([P, PASSES, N], U8, align_bytes=64)
+        b_raw = [sb.tile([P, PACK, N], F32, name="b_raw%d" % z, align_bytes=64) for z in range(PASSES)]
+        bias_col = sb.tile([P, PER], F32)
         ident = sb.tile([P, P], F32, align_bytes=64)
 
-        nc.vector.memset(xs[:].bitcast(I32), 0)
+        nc.vector.memset(x_scales[:].bitcast(I32), 0)
         nc.vector.memset(moved[:].bitcast(I32), 0)
-        nc.gpsimd.memset(was[:].rearrange("p z c -> p (z c)").bitcast(I32), 0)
+        nc.gpsimd.memset(a_planes[:].rearrange("p z c -> p (z c)").bitcast(I32), 0)
         make_identity(nc, ident[:])
 
-        def load_xw(z):
-            nc.sync.dma_start(out=xw[z][:].bitcast(I32), in_=xt_words[z].bitcast(I32))
+        def load_x_words(z):
+            nc.sync.dma_start(out=x_words[z][:].bitcast(I32), in_=xt_words[z].bitcast(I32))
 
-        def load_wb(z):
+        def load_b(z):
             rows = wb[z * P * PACK : (z + 1) * P * PACK, :]
-            nc.sync.dma_start(out=wraw[z][:], in_=rows.rearrange("(p t) n -> p t n", t=PACK))
+            nc.sync.dma_start(out=b_raw[z][:], in_=rows.rearrange("(p t) n -> p t n", t=PACK))
 
-        nc.sync.dma_start(lists[1][:], offs2)
-        load_xw(0)
-        nc.sync.dma_start(lists[0][:], offs)
+        def load_a_scales(quads):
+            for q in quads:
+                nc.sync.dma_start(
+                    out=a_planes[QUAD * q : QUAD * q + ROWS, :, :].bitcast(I32),
+                    in_=wa_scales[:, ROWS * q : ROWS * (q + 1), :].rearrange("z r c -> r z c").bitcast(I32),
+                )
+
+        nc.sync.dma_start(lists[B][:], offs2)
+        load_x_words(0)
+        nc.sync.dma_start(lists[A][:], offs)
         for q in range(QUADS):
             nc.sync.dma_start(
-                out=xs[32 * q : 32 * q + PASSES * ROWS, :].bitcast(I32),
+                out=x_scales[QUAD * q : QUAD * q + PASSES * ROWS, :].bitcast(I32),
                 in_=xt_scales[:, ROWS * q : ROWS * (q + 1), :].bitcast(I32),
             )
-        load_wb(0)
-        nc.sync.dma_start(out=bcol[:], in_=bi.rearrange("o (p c) -> (o p) c", c=2))
-        load_xw(1)
-        load_wb(1)
-        nc.sync.dma_start(out=waw[:].bitcast(I32), in_=wa_words.rearrange("z p c -> p z c").bitcast(I32))
-        for q in range(QUADS):
-            nc.gpsimd.dma_start(
-                out=was[32 * q : 32 * q + ROWS, :, :].bitcast(I32),
-                in_=wa_scales[:, ROWS * q : ROWS * (q + 1), :].rearrange("z r c -> r z c").bitcast(I32),
-            )
+        load_b(0)
+        nc.sync.dma_start(out=bias_col[:], in_=bi.rearrange("o (p c) -> (o p) c", c=PER))
+        load_x_words(1)
+        load_a_scales(range(QUADS // 2))
+        load_b(1)
+        nc.sync.dma_start(out=a_words[:].bitcast(I32), in_=wa_words.rearrange("z p c -> p z c").bitcast(I32))
+        load_a_scales(range(QUADS // 2, QUADS))
 
-        gw = [[None, None], [None, None]]
-        picked = sb.tile([P, 2 * J], U8, align_bytes=64)
-        planes = [picked, moved]
-        wbf = [sb.tile([P, N, PACK], BF16, name="wbf%d" % z, tag="wbf%d" % z, align_bytes=64) for z in range(PASSES)]
-        wq = [sb.tile([P, N], U32, name="wq%d" % z, align_bytes=64) for z in range(PASSES)]
-        wqs = [sb.tile([P, N], U8, name="wqs%d" % z, align_bytes=64) for z in range(PASSES)]
+        picked_words = {}
+        picked_scales = sb.tile([P, 2 * J], U8, align_bytes=64)
+        x_planes = [picked_scales, moved]
+        b_bf16 = [
+            sb.tile([P, N, PACK], BF16, name="b_bf16_%d" % z, tag="b_bf16_%d" % z, align_bytes=64)
+            for z in range(PASSES)
+        ]
+        b_words = [sb.tile([P, N], U32, name="b_words%d" % z, align_bytes=64) for z in range(PASSES)]
+        b_planes = [sb.tile([P, N], U8, name="b_plane%d" % z, align_bytes=64) for z in range(PASSES)]
 
         def gather_words(i, z, tag):
-            gw[i][z] = sb.tile([P, J], U16, name="gw%d%d" % (i, z), tag=tag, align_bytes=64)
-            nc.vector.tensor_copy(gw[i][z][:], xw[z][:].indirect(lists[i][:]))
+            picked = sb.tile([P, J], U16, name="picked%d%d" % (i, z), tag=tag, align_bytes=64)
+            nc.vector.tensor_copy(picked[:], x_words[z][:].indirect(lists[i][:]))
+            picked_words[i, z] = picked
 
-        def round_wb(z):
+        def round_b(z):
             nc.scalar.activation(
-                out=wbf[z][:].rearrange("p (c i) t -> p c t i", i=RUN),
-                in_=wraw[z][:].rearrange("p t (c i) -> p c t i", i=RUN),
+                out=b_bf16[z][:].rearrange("p (c i) t -> p c t i", i=RUN),
+                in_=b_raw[z][:].rearrange("p t (c i) -> p c t i", i=RUN),
                 func=ACT.Copy,
                 scale=-1.0,
             )
 
-        def quantize_wb(z):
+        def quantize_b(z):
             nc.vector.quantize_mx(
-                out=wq[z][:].bitcast(E5M2X4), scales=wqs[z][:], in_=wbf[z][:].rearrange("p n t -> p (n t)")
+                out=b_words[z][:].bitcast(E5M2X4),
+                scales=b_planes[z][:],
+                in_=b_bf16[z][:].rearrange("p n t -> p (n t)"),
             )
 
-        round_wb(0)
-        round_wb(1)
-        gather_words(1, 0, "gw10")
-        for i in range(2):
-            nc.vector.tensor_copy(picked[:, i * J : (i + 1) * J], xs[:].indirect(lists[i][:]))
+        round_b(0)
+        round_b(1)
+        gather_words(B, 0, "picked_b0")
+        for i in (A, B):
+            nc.vector.tensor_copy(picked_scales[:, i * J : (i + 1) * J], x_scales[:].indirect(lists[i][:]))
         for q in range(QUADS):
             nc.sync.dma_start(
-                out=moved[32 * q : 32 * q + ROWS, :].bitcast(I32),
-                in_=picked[32 * q + ROWS : 32 * q + 2 * ROWS, :].bitcast(I32),
+                out=moved[QUAD * q : QUAD * q + ROWS, :].bitcast(I32),
+                in_=picked_scales[QUAD * q + ROWS : QUAD * q + 2 * ROWS, :].bitcast(I32),
             )
-        gather_words(0, 0, "xs")
-        quantize_wb(0)
-        gather_words(0, 1, "wbf0")
-        gather_words(1, 1, "gw11")
-        quantize_wb(1)
+        gather_words(A, 0, "x_scales")
+        quantize_b(0)
+        gather_words(A, 1, "b_bf16_0")
+        gather_words(B, 1, "picked_b1")
+        quantize_b(1)
 
-        bias_ps = ps.tile([P, 2, P], F32)
-        for c in range(2):
-            nc.tensor.transpose(bias_ps[:, c, :], bcol[:, c : c + 1].to_broadcast([P, P]), ident[:])
-        bias = sb.tile([P, P, 2], F32)
-        nc.scalar.activation(out=bias[:], in_=bias_ps[:].rearrange("p c k -> p k c"), func=ACT.Copy, scale=GAP)
+        bias_ps = ps.tile([P, PER, P], F32)
+        for c in range(PER):
+            nc.tensor.transpose(bias_ps[:, c, :], bias_col[:, c : c + 1].to_broadcast([P, P]), ident[:])
+        bias = sb.tile([P, P, PER], F32)
+        nc.scalar.activation(
+            out=bias[:], in_=bias_ps[:].rearrange("p c k -> p k c"), func=ACT.Copy, scale=GAP_SCALE
+        )
 
-        gap = [ps.tile([P, N], F32, name="gap%d" % h) for h in range(J // P)]
-        steps = [(1, 0), (0, 0), (0, 1), (1, 1)]
+        gap = [ps.tile([P, N], F32, name="gap%d" % h) for h in range(TILES)]
+        steps = [(B, 0), (A, 0), (A, 1), (B, 1)]
         for s, (i, z) in enumerate(steps):
-            for h in range(J // P):
-                cols = slice(h * P, (h + 1) * P)
-                if i == 0:
-                    rhs, rhs_scale = waw[:, z, :].bitcast(FP4X4), was[:, z, :]
+            for h in range(TILES):
+                if i == A:
+                    rhs, rhs_scale = a_words[:, z, :].bitcast(FP4X4), a_planes[:, z, :]
                 else:
-                    rhs, rhs_scale = wq[z][:].bitcast(E5M2X4), wqs[z][:]
+                    rhs, rhs_scale = b_words[z][:].bitcast(E5M2X4), b_planes[z][:]
                 nc.tensor.matmul_mx(
                     out=gap[h][:],
-                    lhsT=gw[i][z][:, cols].bitcast(FP4X4),
-                    lhsT_scale=planes[z][:, i * J + h * P : i * J + (h + 1) * P],
+                    lhsT=picked_words[i, z][:, h * P : (h + 1) * P].bitcast(FP4X4),
+                    lhsT_scale=x_planes[z][:, i * J + h * P : i * J + (h + 1) * P],
                     rhs=rhs,
                     rhs_scale=rhs_scale,
                     start=(s == 0),
                     stop=(s == len(steps) - 1),
                 )
 
-        neg = [sb.tile([P, N], F32, name="neg%d" % h) for h in range(J // P)]
-        low = [sb.tile([P, 1], F32, name="low%d" % h) for h in range(J // P)]
-        for h in range(J // P):
+        neg = [sb.tile([P, N], F32, name="neg%d" % h) for h in range(TILES)]
+        low = [sb.tile([P, 1], F32, name="low%d" % h) for h in range(TILES)]
+        for h in range(TILES):
             nc.vector.scalar_tensor_tensor(
-                out=neg[h][:], in0=gap[h][:], scalar=-GAP, in1=bias[:].rearrange("p k c -> p (k c)"),
-                op0=ALU.mult, op1=ALU.add,
+                out=neg[h][:],
+                in0=gap[h][:],
+                scalar=-GAP_SCALE,
+                in1=bias[:].rearrange("p k c -> p (k c)"),
+                op0=ALU.mult,
+                op1=ALU.add,
             )
-        for h in range(J // P):
+        for h in range(TILES):
             nc.vector.tensor_reduce(out=low[h][:], in_=neg[h][:], axis=mybir.AxisListType.X, op=ALU.min)
-        for h in range(J // P):
+        for h in range(TILES):
             e = sb.tile([P, N], F32, name="e%d" % h)
             total = sb.tile([P, 1], F32, name="total%d" % h)
             inv = sb.tile([P, 1], F32, name="inv%d" % h)
-            y = sb.tile([P, N], F32, name="y%d" % h)
-            nc.scalar.activation(out=e[:], in_=neg[h][:], func=ACT.Exp, bias=low[h][:], scale=-1.0, accum_out=total[:])
+            shares = sb.tile([P, N], F32, name="shares%d" % h)
+            nc.scalar.activation(
+                out=e[:], in_=neg[h][:], func=ACT.Exp, bias=low[h][:], scale=-1.0, accum_out=total[:]
+            )
             nc.vector.reciprocal(out=inv[:], in_=total[:])
-            nc.vector.tensor_scalar(out=y[:], in0=e[:], scalar1=inv[:], scalar2=TOTAL, op0=ALU.mult, op1=ALU.mult)
-            nc.sync.dma_start(out=out[h * P : (h + 1) * P, :], in_=y[:])
+            nc.vector.tensor_scalar(
+                out=shares[:], in0=e[:], scalar1=inv[:], scalar2=SHARE_SUM, op0=ALU.mult, op1=ALU.mult
+            )
+            nc.sync.dma_start(out=out[h * P : (h + 1) * P, :], in_=shares[:])

from contextlib import ExitStack

import concourse.mybir as mybir
from concourse.masks import make_identity

K, T, J, N = 1024, 1024, 256, 256
FLOPS = 2 * 2 * K * J * N

F32 = mybir.dt.float32
BF16 = mybir.dt.bfloat16
I32 = mybir.dt.int32
U32 = mybir.dt.uint32
U16 = mybir.dt.uint16
U8 = mybir.dt.uint8
FP4X4 = mybir.dt.float4_e2m1fn_x4
E5M2X4 = mybir.dt.float8_e5m2_x4
ALU = mybir.AluOpType
ACT = mybir.ActivationFunctionType

P = 128
PACK = 4
PASSES = K // (P * PACK)
QUAD = 32
QUADS = P // QUAD
ROWS = 4
RUN = 4
PER = N // P
TILES = J // P
A, B = 0, 1
GAP_SCALE = 0.6
SHARE_SUM = 256.0


def tile_list_rows_twotokens_sharesofgap_kernel(
    tc, xt_words, xt_scales, wa_words, wa_scales, wb, bi, offs, offs2, out
):
    nc = tc.nc
    with ExitStack() as ctx:
        sb = ctx.enter_context(tc.tile_pool(name="sb", bufs=1))
        ps = ctx.enter_context(tc.psum_pool(name="ps", bufs=1))

        lists = [sb.tile([P, J // 16], U16, name="list%d" % i) for i in (A, B)]
        x_words = [sb.tile([P, T], U16, name="x_words%d" % z, align_bytes=64) for z in range(PASSES)]
        x_scales = sb.tile([P, T], U8, tag="x_scales", align_bytes=64)
        moved = sb.tile([P, 2 * J], U8, align_bytes=64)
        a_words = sb.tile([P, PASSES, 2 * N], U8, align_bytes=64)
        a_planes = sb.tile([P, PASSES, N], U8, align_bytes=64)
        b_raw = [sb.tile([P, PACK, N], F32, name="b_raw%d" % z, align_bytes=64) for z in range(PASSES)]
        bias_col = sb.tile([P, PER], F32)
        ident = sb.tile([P, P], F32, align_bytes=64)

        nc.vector.memset(x_scales[:].bitcast(I32), 0)
        nc.vector.memset(moved[:].bitcast(I32), 0)
        nc.gpsimd.memset(a_planes[:].rearrange("p z c -> p (z c)").bitcast(I32), 0)
        make_identity(nc, ident[:])

        def load_x_words(z):
            nc.sync.dma_start(out=x_words[z][:].bitcast(I32), in_=xt_words[z].bitcast(I32))

        def load_b(z):
            rows = wb[z * P * PACK : (z + 1) * P * PACK, :]
            nc.sync.dma_start(out=b_raw[z][:], in_=rows.rearrange("(p t) n -> p t n", t=PACK))

        def load_a_scales(quads):
            for q in quads:
                nc.sync.dma_start(
                    out=a_planes[QUAD * q : QUAD * q + ROWS, :, :].bitcast(I32),
                    in_=wa_scales[:, ROWS * q : ROWS * (q + 1), :].rearrange("z r c -> r z c").bitcast(I32),
                )

        nc.sync.dma_start(lists[B][:], offs2)
        load_x_words(0)
        nc.sync.dma_start(lists[A][:], offs)
        for q in range(QUADS):
            nc.sync.dma_start(
                out=x_scales[QUAD * q : QUAD * q + PASSES * ROWS, :].bitcast(I32),
                in_=xt_scales[:, ROWS * q : ROWS * (q + 1), :].bitcast(I32),
            )
        load_b(0)
        nc.sync.dma_start(out=bias_col[:], in_=bi.rearrange("o (p c) -> (o p) c", c=PER))
        load_x_words(1)
        load_a_scales(range(QUADS // 2))
        load_b(1)
        nc.sync.dma_start(out=a_words[:].bitcast(I32), in_=wa_words.rearrange("z p c -> p z c").bitcast(I32))
        load_a_scales(range(QUADS // 2, QUADS))

        picked_words = {}
        picked_scales = sb.tile([P, 2 * J], U8, align_bytes=64)
        x_planes = [picked_scales, moved]
        b_bf16 = [
            sb.tile([P, N, PACK], BF16, name="b_bf16_%d" % z, tag="b_bf16_%d" % z, align_bytes=64)
            for z in range(PASSES)
        ]
        b_words = [sb.tile([P, N], U32, name="b_words%d" % z, align_bytes=64) for z in range(PASSES)]
        b_planes = [sb.tile([P, N], U8, name="b_plane%d" % z, align_bytes=64) for z in range(PASSES)]

        def gather_words(i, z, tag):
            picked = sb.tile([P, J], U16, name="picked%d%d" % (i, z), tag=tag, align_bytes=64)
            nc.vector.tensor_copy(picked[:], x_words[z][:].indirect(lists[i][:]))
            picked_words[i, z] = picked

        def round_b(z):
            nc.scalar.activation(
                out=b_bf16[z][:].rearrange("p (c i) t -> p c t i", i=RUN),
                in_=b_raw[z][:].rearrange("p t (c i) -> p c t i", i=RUN),
                func=ACT.Copy,
                scale=-1.0,
            )

        def quantize_b(z):
            nc.vector.quantize_mx(
                out=b_words[z][:].bitcast(E5M2X4),
                scales=b_planes[z][:],
                in_=b_bf16[z][:].rearrange("p n t -> p (n t)"),
            )

        round_b(0)
        round_b(1)
        gather_words(B, 0, "picked_b0")
        for i in (A, B):
            nc.vector.tensor_copy(picked_scales[:, i * J : (i + 1) * J], x_scales[:].indirect(lists[i][:]))
        for q in range(QUADS):
            nc.sync.dma_start(
                out=moved[QUAD * q : QUAD * q + ROWS, :].bitcast(I32),
                in_=picked_scales[QUAD * q + ROWS : QUAD * q + 2 * ROWS, :].bitcast(I32),
            )
        gather_words(A, 0, "x_scales")
        quantize_b(0)
        gather_words(A, 1, "b_bf16_0")
        gather_words(B, 1, "picked_b1")
        quantize_b(1)

        bias_ps = ps.tile([P, PER, P], F32)
        for c in range(PER):
            nc.tensor.transpose(bias_ps[:, c, :], bias_col[:, c : c + 1].to_broadcast([P, P]), ident[:])
        bias = sb.tile([P, P, PER], F32)
        nc.scalar.activation(
            out=bias[:], in_=bias_ps[:].rearrange("p c k -> p k c"), func=ACT.Copy, scale=GAP_SCALE
        )

        gap = [ps.tile([P, N], F32, name="gap%d" % h) for h in range(TILES)]
        steps = [(B, 0), (A, 0), (A, 1), (B, 1)]
        for s, (i, z) in enumerate(steps):
            for h in range(TILES):
                if i == A:
                    rhs, rhs_scale = a_words[:, z, :].bitcast(FP4X4), a_planes[:, z, :]
                else:
                    rhs, rhs_scale = b_words[z][:].bitcast(E5M2X4), b_planes[z][:]
                nc.tensor.matmul_mx(
                    out=gap[h][:],
                    lhsT=picked_words[i, z][:, h * P : (h + 1) * P].bitcast(FP4X4),
                    lhsT_scale=x_planes[z][:, i * J + h * P : i * J + (h + 1) * P],
                    rhs=rhs,
                    rhs_scale=rhs_scale,
                    start=(s == 0),
                    stop=(s == len(steps) - 1),
                )

        neg = [sb.tile([P, N], F32, name="neg%d" % h) for h in range(TILES)]
        low = [sb.tile([P, 1], F32, name="low%d" % h) for h in range(TILES)]
        for h in range(TILES):
            nc.vector.scalar_tensor_tensor(
                out=neg[h][:],
                in0=gap[h][:],
                scalar=-GAP_SCALE,
                in1=bias[:].rearrange("p k c -> p (k c)"),
                op0=ALU.mult,
                op1=ALU.add,
            )
        for h in range(TILES):
            nc.vector.tensor_reduce(out=low[h][:], in_=neg[h][:], axis=mybir.AxisListType.X, op=ALU.min)
        for h in range(TILES):
            e = sb.tile([P, N], F32, name="e%d" % h)
            total = sb.tile([P, 1], F32, name="total%d" % h)
            inv = sb.tile([P, 1], F32, name="inv%d" % h)
            shares = sb.tile([P, N], F32, name="shares%d" % h)
            nc.scalar.activation(
                out=e[:], in_=neg[h][:], func=ACT.Exp, bias=low[h][:], scale=-1.0, accum_out=total[:]
            )
            nc.vector.reciprocal(out=inv[:], in_=total[:])
            nc.vector.tensor_scalar(
                out=shares[:], in0=e[:], scalar1=inv[:], scalar2=SHARE_SUM, op0=ALU.mult, op1=ALU.mult
            )
            nc.sync.dma_start(out=out[h * P : (h + 1) * P, :], in_=shares[:])
